import numpy as np, ml_dtypes
CORES = [23,119,17,113]
N = 4
BF = ml_dtypes.bfloat16
P, CAP, J, W, D, RO = 512, 128, 8, 8192, 3, 9
WT = np.array([1, 3, 7, 13, 21, 35, 49, 67, 85, 107, 129, 155, 181, 211, 241, 253], np.int32)
KA = np.array([17, 101, 263, 389, 547, 701, 859, 1021], np.int32)
def mark(s):
    return np.add.reduce(s * WT[:, None], axis=-2) & 4095
def columns(u, e):
    return ((u * u >> 4)[..., None, :] + KA[:, None] * u[..., None, :] + 811 * e) & (W - 1)
def lanes(rng, v, k):
    return np.minimum((rng.random((N, 8, 16, k), dtype=np.float32) * (v + 1)[:, None, None]).astype(np.int32), v[:, None, None])
def toward(s, r):
    z = np.array(s); z[0] = (s[0] & (64 - N)) + ((s[0] + r - mark(s)) & (N - 1))
    return z
def pack(o, s, c):
    return {"opr": np.ascontiguousarray(o.reshape(N, 128, W)).astype(np.float32).astype(BF), "s0": np.ascontiguousarray(s.reshape(N, 128, P)).astype(np.float32).astype(BF),
            "f0": np.ascontiguousarray(c).astype(np.int32)}
def setup_inputs(rng):
    t = rng.permutation(8); v = np.full(8, 63); v[t[0]] = rng.choice(np.array([1, 3])); v[t[1]] = 15
    span = rng.choice(np.array([40, 100, 200, 400]), (8, 1)); span[t[0]] = 1
    c = (rng.random((N, 8, P)) * (span + 1)).astype(np.int64)
    c = np.where(rng.random((N, 8, P)) < rng.choice(np.array([0.0, 0.1, 0.3]), (N, 8, 1)), 1023, c)
    return pack(lanes(rng, v, W), lanes(rng, v, P), c)
def setup_inputs_spread(rng):
    o = np.minimum((np.exp2(6 * rng.random((N, 8, 1, W))) * rng.random((N, 8, 16, W))).astype(np.int64), 63)
    s = np.minimum((np.exp2(6 * rng.random((N, 8, 1, P))) * rng.random((N, 8, 16, P))).astype(np.int64), 63)
    c = np.minimum(np.exp2(10 * rng.random((N, 8, P))).astype(np.int64) - 1, 1022)
    return pack(o, s, np.where(rng.random((N, 8, P)) < 0.125, 1023, c))
def setup_inputs_ends(rng):
    o = 63 * rng.integers(0, 2, (N, 8, 16, W)); s = 63 * rng.integers(0, 2, (N, 8, 16, P))
    share = rng.permutation(np.array([1.0, 1.0, 1.0, 0.9, 0.7, 0.5, 0.3, 0.1]))
    c = np.where(rng.random((N, 8, P)) < share[:, None], 0, 1023)
    m = 63 * ((np.arange(65536)[:, None] >> np.arange(16)) & 1)
    u = np.arange(4096); free = np.zeros((4096, 16), np.int64)
    free[:, 15] = u // 253; free[:, 4] = (u % 253) // 21; free[:, 0] = (u % 253) % 21
    every = columns(mark(free.T), 0)
    for k, x in ((P - 3, int(np.max(every))), (P // 2, int(np.min(every)))):
        for b in (m, free):
            z = np.nonzero(np.any(columns(mark(b.T), 0) == x, axis=0))[0]
            if len(z):
                s[:, :, :, k] = b[rng.choice(z, (N, 8))]; c[:, :, k] = 0
                break
    s[..., [0, 1, P - 2, P - 1]] = 63; c[..., [0, P - 1]] = 0; c[..., [1, P - 2]] = 1023
    a = columns(mark(np.full((16, 1), 63)), 0)[:, 0]
    o[..., a[0]] = 0; o[..., a[J - 1]] = 63
    return pack(o, s, c)
def setup_inputs_corners(rng):
    t = rng.permutation(8); v = np.full(8, 63); v[t[6]] = 1; v[t[7]] = 7
    o = lanes(rng, v, W); s = lanes(rng, v, P); c = np.full((N, 8, P), 1023); n = CAP // J; big = int(rng.integers(0, N))
    o[:, t[7]] = 0; c[:, t[0]] = 0; c[N - 1, t[2], P - 1] = 0
    c[:, t[6]] = rng.integers(1012, 1024, (N, P)); c[:, t[7]] = rng.integers(0, 101, (N, P))
    a = columns(mark(np.full((16, 1), 63)), 0)[:, 0]
    for q in range(N):
        for k in (3, 4, 5):
            g = int(t[k]); x = rng.integers(0, 16, 16); x[0] = 0
            x[0] = (q + 1 - int(mark(x[:, None])[0])) & (N - 1)
            o[q, g][:, a] = (63 - x)[:, None]; b = 300 - (int(np.add.reduce(x)) >> 2)
            if k == 5: c[q, g] = np.where(rng.random(P) < 0.5, rng.integers(400, 700, P), 1023)
            w = n + k - 3 if k < 5 else n + 1 if q == big else int(rng.integers(0, n + 1))
            p = np.append(P - 1, rng.permutation(P - 1))[:w]
            s[q, g][:, p] = 63; c[q, g, p] = b
            if k == 4: c[q, g, p[-1]] = b + 1
    return pack(o, s, c)
def setup_inputs_edges(rng):
    t = [int(k) for k in rng.permutation(8)]; v = np.full(8, 63); v[t[7]] = 15
    n = CAP // J; r = int(rng.integers(0, N)); big = int(rng.integers(0, N)); top = int(rng.integers(520, 1001))
    o = lanes(rng, v, W); s = lanes(rng, v, P)
    c = (rng.random((N, 8, P)) * rng.choice(np.array([41, 101, 201]), (8, 1))).astype(np.int64)
    c = np.where(rng.random((N, 8, P)) < 0.1, 1023, c)
    o[:, t[:3]] = 0; c[:, t[0]] = rng.integers(1, 201, (N, P)); c[:, t[1:5]] = 1023
    for q in range(N):
        for k in range(3):
            w = n if k == 1 else n + (k == 0) if q == big else int(rng.integers(0, n + 1))
            p = np.append(P - 1, rng.permutation(P - 1))[:w]
            z = toward(s[q, t[k]][:, p], r)
            if k == 0: z = 0 * z
            s[q, t[k]][:, p] = z; h = np.add.reduce(z, axis=0) >> 2
            if k == 0: c[q, t[k], p] = 0
            elif k == 1: c[q, t[k], p] = top + np.arange(q * n, q * n + n) * 8 // (N * n) - 2 * h
            else: c[q, t[k], p] = 1022 - 2 * h
    for k in (3, 4):
        x = t[k]; z = rng.integers(1, 8, 16); z[0] += (2 - int(mark(z[:, None])[0])) & 3
        h = int(np.add.reduce(z)) >> 2; o[:, x] = rng.integers(56, 64, (N, 16, W))
        for e in range(D): o[:, x, :, int(columns(mark(z[:, None]), e)[0, 0])] = 0
        q = rng.permutation(N); a = int(q[0]); p = np.append(P - 1, rng.permutation(P - 1))[:CAP + 1]
        if k == 3: b = int(q[1]); low = 1022 - 3 * h; more = 1
        else: b = a; low = int(rng.integers(850, 911)); more = h
        s[a, x][:, p[1:]] = z[:, None]; c[a, x, p[1:]] = low + more
        s[b, x, :, P - 1] = z; c[b, x, P - 1] = low
    return pack(o, s, c)
def setup_inputs_ties(rng):
    v = rng.permutation(np.array([1, 1, 3, 3, 7, 15, 31, 63])); o = lanes(rng, v, W); s = lanes(rng, v, P)
    c = rng.choice(np.array([0, 5, 9]), (1, 8, 1)) + rng.integers(0, 2, (N, 8, P)) * rng.choice(np.array([0, 1, 3]), (1, 8, 1))
    s[:, 1::2, :, P // 2:] = s[:, 1::2, :, :P // 2]
    c = np.where(rng.random((N, 8, P)) < 0.05, 1023, c)
    x = int(np.nonzero(v == 1)[0][0]); y = int(np.nonzero(v == 3)[0][0])
    o[:, x] = 0; c[:, x] = 1023
    s[:, x] = rng.integers(0, 64, (N, 16, P)); s[:, x, 0] = np.maximum(s[:, x, 0], 4)
    for q in range(N):
        p = np.append(P - 1, rng.permutation(P - 1))[:CAP // J]
        a = np.add.reduce(s[q, x][:, p], axis=0) >> 2
        c[q, x, p] = 1022 - a - rng.integers(0, a)
    z = rng.integers(1, 8, 16); z[0] += (2 - int(mark(z[:, None])[0])) & 3
    a = int(np.add.reduce(z)) >> 2; b = int(rng.integers(850, 931))
    o[:, y] = rng.integers(56, 64, (N, 16, W)); c[:, y] = 1023
    for e in range(D): o[:, y, :, int(columns(mark(z[:, None]), e)[0, 0])] = 0
    q = rng.permutation(N); p = rng.permutation(P)[:CAP]
    s[int(q[0]), y][:, p] = z[:, None]; c[int(q[0]), y, p] = b + a
    s[int(q[1]), y, :, P - 1] = z; c[int(q[1]), y, P - 1] = b
    return pack(o, s, c)
def check_inputs(d):
    bad = []
    for k, lo, hi in (("opr", 0, 63), ("s0", 0, 63), ("f0", 0, 1023)):
        x = np.asarray(d[k]).astype(np.float64)
        if not (np.min(x) >= lo and np.max(x) <= hi): bad.append("range of " + k)
        elif np.any(x != np.floor(x)): bad.append("whole numbers of " + k)
    return bad
def reference(opr, s0, f0):
    o = opr.astype(np.float32).astype(np.int32).reshape(N, 8, 16, W); gi = np.arange(8)
    S = np.zeros((N, 8, D + 1, 16, P), np.int32); F = np.full((N, 8, D + 1, P), 1023, np.int32)
    S[:, :, 0] = s0.astype(np.float32).astype(np.int32).reshape(N, 8, 16, P); F[:, :, 0] = f0
    lo = np.zeros((8, D), np.int32); hi = np.zeros((8, D), np.int32); U = np.full(8, 1023, np.int32); lev = np.zeros(8, np.int32)
    for rnd in range(RO):
        s = S[:, gi, lev]; f = F[:, gi, lev]; low = lo[gi, lev][:, None]
        h = columns(mark(s), lev[:, None, None]).reshape(N, 8, 1, J * P)
        c = np.abs(np.tile(s, (1, 1, 1, J)) - np.take_along_axis(o, h.astype(np.int64), axis=3))
        fc = np.tile(f, (1, 1, J)) + (np.add.reduce(c, axis=2) >> 2); own = mark(c) & (N - 1)
        B = np.full(8, 1023, np.int32)
        for a in range(N):
            x = np.partition(np.where((fc >= low) & (own == a), fc, 4000), CAP, axis=2)[:, :, CAP]
            B = np.minimum(B, np.min(x, axis=0))
        keep = (fc >= low) & (fc < B[:, None])
        m = np.min(np.where(keep, fc, 4000), axis=(0, 2))
        ns = np.zeros((N, 8, 16, P), np.int32); nf = np.full((N, 8, P), 1023, np.int32)
        for a in range(N):
            k = keep & (own == a); place = np.add.accumulate(k, axis=2, dtype=np.int64) - 1
            qi, ji, ci = np.nonzero(k); t = qi * CAP + place[qi, ji, ci]
            ns[a, ji, :, t] = c[qi, ji, :, ci]; nf[a, ji, t] = fc[qi, ji, ci]
        S[:, gi, lev + 1] = ns; F[:, gi, lev + 1] = nf; hi[gi, lev] = B
        U = np.where(lev == D - 1, np.minimum(U, m), U)
        for g in range(8):
            e = int(lev[g])
            if e == D - 1 or m[g] >= U[g]:
                lo[g, e] = max(int(B[g]), int(lo[g, e]) + 1)
                if lo[g, e] >= U[g] and e > 0:
                    lo[g, e] = 0; e -= 1; lo[g, e] = max(int(hi[g, e]), int(lo[g, e]) + 1)
            else:
                e += 1; lo[g, e] = 0
            lev[g] = e
    yl = np.ascontiguousarray(S[:, :, 1:].transpose(0, 1, 3, 2, 4)).reshape(N, 128, D * P)
    yt = np.concatenate([lo, hi, lev[:, None], U[:, None]], axis=1)
    return {"yl": yl.astype(np.float32).astype(BF), "yf": np.ascontiguousarray(F[:, :, 1:]).reshape(N, 8, D * P).astype(np.float32), "yt": np.stack([yt] * N).astype(np.float32)}

from concourse.bass import DstId, RemoteDMATransfer
from concourse.mybir import AluOpType as A, AxisListType, ActivationFunctionType as F

RO = 9
NSLOT = RO + 2
KA = [17, 101, 263, 389, 547, 701, 859, 1021]
WTS = [1, 3, 7, 13, 21, 35, 49, 67, 85, 107, 129, 155, 181, 211, 241, 253]
CW = 4112

SCRATCH = {"PS": ("psum", [128, 4096], "float32")}
for _dt, _names in (
        ("bfloat16", "OPS:8192 CH:4112 FB:4112 DY:4096 SS:512 SF:512 IN0:1024 SC:1024 DD:1024 STEP:1024 IND:4096 CCR:512 MSG:1024 CN:32"
                     " TLM:128 WMARK:144 WF0:144 WF1:144 SEL4:16 MASKG:16 IDENT:128 ONES:128 TRI:128 SHIFT:128 IMS:128 CS0:128 CS1:128"
                     " CM:128 QALL:128 LANEG:128 BO:128 BCF:128 BLK:128 TMPA:128 TMPB:128 DIAG:2048 KK:512 RST:512 OWF:256"),
        ("float16", "KEY:1024 RH:4 BH:4 WT0:160 WT1:160"),
        ("float32", "BML:144 UF:64 KU:256 KMAT:256 PEN:256 CC:256 CP:256 SG:32 SELC:64 SP:16 TS:4 MT:32 MTT:32 MM:4 ST:16 LT:128"
                    " COL:32 WROW:48 LQ:16 HM:2 I3:8 PWC:32 K1:32 K2:32 YT:8 PW0:32 PW1:32 PW2:32 RE0:16 WX:192"),
        ("int32", "FL:512 UI:128 OFP:256 OFM:256 LI:64 I1:256 OW:256 T4:256 CI:160 C5:128 C4:128 CL:128 RF:132 RF2:132 CM3:16 TI:8 WI:4"
                  " F0:512 FH:512 FD:512 FE:512 FG:512"),
        ("uint16", "OFU:256 OFS:32 LU:32 LCU:32 REP:16")):
    for _n in _names.split():
        _n, _c = _n.split(":")
        SCRATCH[_n] = ("sbuf", [128, int(_c)], _dt)
SCRATCH["XF"] = ("sbuf", [128, NSLOT * 1024], "bfloat16")
for _l in (1, 2, 3):
    for _n, _c, _dt in (("FS", 512, "bfloat16"), ("FC", 512, "bfloat16"), ("FV", 512, "float32"), ("FA", 512, "bfloat16"),
                        ("FN", 512, "bfloat16"), ("FO", 64, "uint16"), ("OS", 1024, "bfloat16"), ("OV", 1024, "float32")):
        SCRATCH[_n + str(_l)] = ("sbuf", [128, _c], _dt)

SEMAPHORES = (["qV", "qS", "qP", "qG", "ld0", "ld1", "ld2", "out", "lsb", "lsd"]
              + ["bm%d" % r for r in range(RO)] + ["dat%d" % r for r in range(RO)])


def rank_program(g, core, T, topo):
    rank = T.rank_of(core)
    if rank is None:
        return
    cores = list(T.cores)
    eng = {"V": g.vector, "S": g.scalar, "P": g.tensor, "G": g, "Y": g.sync}
    qs = {"V": "qV", "S": "qS", "P": "qP", "G": "qG"}
    cnt, snap, lastw, readers = {}, {}, {}, {}
    known = {q: {} for q in eng}

    def need(q, toks):
        best = {}
        for s, v in toks:
            if known[q].get(s, 0) < v:
                best[s] = max(best.get(s, 0), v)
        for s in sorted(best):
            v = best[s]
            if known[q].get(s, 0) < v:
                eng[q].wait_ge(T.sem[s], v)
                known[q][s] = v
                for s2, v2 in snap.get((s, v), {}).items():
                    known[q][s2] = max(known[q].get(s2, 0), v2)

    def deps(q, r, w):
        own = qs.get(q)
        toks = []
        for k in r:
            if k in lastw:
                toks.append(lastw[k])
            if k[:2] == "ps":
                toks += [t for t in readers.get(k, {}).items() if t[0] != own]
        for k in w:
            k, more = k.rstrip("+"), k[-1] == "+" or k[:2] == "ps"
            if k in lastw and not (more and lastw[k][0] == own):
                toks.append(lastw[k])
            toks += readers.get(k, {}).items()
        return toks

    def mark(q, tok, r, w):
        snap[tok] = dict(known[q])
        for k in r:
            readers.setdefault(k, {})[tok[0]] = tok[1]
        for k in w:
            k = k.rstrip("+")
            lastw[k] = tok
            readers[k] = {}

    def do(q, f, r, w):
        r, w = r.split(), w.split()
        need(q, deps(q, r, w))
        s = qs[q]
        f(eng[q]).then_inc(T.sem[s], 1)
        cnt[s] = cnt.get(s, 0) + 1
        mark(q, (s, cnt[s]), r, w)

    def dma(q, sem, pairs, r, w):
        r, w = r.split(), w.split()
        need(q, deps(q, r, w))
        for out, in_ in pairs:
            eng[q].dma_start(out, in_).then_inc(T.sem[sem], 16)
            cnt[sem] = cnt.get(sem, 0) + 16
        mark(q, (sem, cnt[sem]), r, w)

    def V(f, r, w):
        do("V", f, r, w)

    def ts(r, w, out, i, s1, o0, s2=None, o1=None):
        if o1 is None:
            V(lambda e: e.tensor_scalar(out, i, s1, None, o0), r, w)
        else:
            V(lambda e: e.tensor_scalar(out, i, s1, s2, o0, o1), r, w)

    def tt(r, w, out, a, b_, op):
        V(lambda e: e.tensor_tensor(out, a, b_, op), r, w)

    def cp(r, w, out, i):
        V(lambda e: e.tensor_copy(out, i), r, w)

    def red(r, w, out, i, op):
        V(lambda e: e.tensor_reduce(out, i, AxisListType.X, op), r, w)

    def fill(w, out, c):
        V(lambda e: e.memset(out, c), "", w)

    def scan(r, w, out, i):
        V(lambda e: e.tensor_tensor_scan(out, T.RST[:], i, 0.0, A.mult, A.add), r, w)

    def mm(r, w, out, l, r_, st=True, sp=True):
        do("P", lambda e: e.matmul(out, l, r_, st, sp), r, w)

    def act(r, w, out, i, fn, **k):
        do("S", lambda e: e.activation(out, i, fn, **k), r, w)

    def b(k, x, y, st=1):
        return T.PS[:, k * 512 + x:k * 512 + y:st] if st > 1 else T.PS[:, k * 512 + x:k * 512 + y]

    def plan(src):
        off = [c for c in cores if topo.chip(c) != topo.chip(src)]
        on = [c for c in cores if topo.chip(c) == topo.chip(src) and c != src]
        base = list(topo.engines(src, off[0]))
        rest = [e for e in topo.engines(src, on[0]) if e not in base]
        out = {}
        for cs, es in ((off, base), (on, rest)):
            p = len(es) // len(cs)
            for i, c in enumerate(cs):
                out[c] = es[i * p:(i + 1) * p]
        return out

    mine = plan(core)
    arrive = sum(len(plan(c)[core]) for c in cores if c != core)

    def send(name, r, local, src_of, dst, keys):
        keys = keys.split()
        need("G", deps("G", keys, []))
        tr = []
        for c, en in mine.items():
            rid, pid, _ = topo.addr(c)
            tr.append(RemoteDMATransfer(dst_ids=[DstId(rid=rid, pnc=pid)], dma_engine_mask=sum(1 << e for e in en),
                                        remote_sem=T.sem["%s%d" % (name, r)], srcs=[src_of(cores.index(c))], dsts=[dst]))
        g.remote_dma_fused(tr, local_sem=T.sem[local])
        cnt[local] = cnt.get(local, 0) + sum(len(en) for en in mine.values())
        mark("G", (local, cnt[local]), keys, [])
        lastw["%s%d" % (name, r)] = ("%s%d" % (name, r), arrive)

    fill("F0", T.F0[:], 0)
    dma("S", "ld0", [(T.XF[:, q * 256:q * 256 + 128], T.s0[:, q * 128:(q + 1) * 128]) for q in range(4)], "", "XF0s")
    dma("S", "ld1", [(T.F0[0::16, :], T.f0[:]), (T.F0[1::16, :], T.f0[:])], "", "F0")
    dma("Y", "ld2", [(T.OPS[:], T.opr[:])], "", "OPS")

    def iota(w, out, pat, base=0, cm=0, small=False):
        if small:
            do("G", lambda e: e.iota(out, pat, base, cm, allow_small_or_imprecise_dtypes=True), "", w)
        else:
            do("G", lambda e: e.iota(out, pat, base, cm), "", w)

    iota("TI", T.TI[:, 0:1], [[1, 1]], 0, 1)
    iota("CI", T.CI[:], [[1, 160]])
    iota("PW0", T.PW0[:], [[256, 4], [16, 8]], small=True)
    iota("RF", T.RF[:], [[1, 33], [1000, 4]], -3000)
    iota("CM3", T.CM3[:], [[0, 4], [1, 4]])
    iota("RE0", T.RE0[:], [[0, 8], [16, 2]], small=True)
    iota("C4", T.C4[:], [[1, 8], [0, 16]])
    iota("CL", T.CL[:], [[0, 8], [1, 16]])
    iota("C5", T.C5[:], [[1, 4], [0, 32]])
    iota("KK", T.KK[:], [[0, 4], [1, 16], [16, 8]], small=True)
    iota("PW1", T.PW1[:], [[0, 4], [16, 8]], small=True)
    iota("PW2", T.PW2[:], [[16, 32]], small=True)

    def C(k):
        return T.COL[:, k:k + 1]
    cp("TI", "c0", C(0), T.TI[:, 0:1])
    for k, sh, an in ((1, 0, 15), (2, 4, 7), (3, 0, 31), (4, 5, 3), (6, 4, 1)):
        ts("TI", "TI%d" % k, T.TI[:, k:k + 1], T.TI[:, 0:1], sh, A.logical_shift_right, an, A.bitwise_and)
    for k in (1, 2, 3, 4, 6):
        cp("TI%d" % k, "c%d" % k, C(k), T.TI[:, k:k + 1])
    for i in range(16):
        fill("wr+", T.WROW[:, i:i + 1], WTS[i])
    ts("CI c1", "wm", T.WROW[:, 16:32], T.CI[:, 0:16], C(1), A.is_equal)
    tt("wr wm", "wx", T.WROW[:, 32:48], T.WROW[:, 0:16], T.WROW[:, 16:32], A.mult)
    red("wx", "c7", C(7), T.WROW[:, 32:48], A.add)
    tt("c0 c1", "c12", C(12), C(0), C(1), A.subtract)
    ts("c12", "c13", C(13), C(12), 15.0, A.add)
    ts("CI c13 c7", "WMARK", T.WMARK[:, 0:143], T.CI[:, 0:143], C(13), A.is_equal, C(7), A.mult)
    ts("PW0 c1", "PWC", T.PWC[:], T.PW0[:], C(1), A.add)
    ts("RE0 c1", "REP", T.REP[:], T.RE0[:], C(1), A.add)
    for j in range(8):
        fill("KMAT+", T.KMAT[:, j * 32:(j + 1) * 32], KA[j])
    cp("c7", "wi0", T.WI[:, 0:1], C(7))
    ts("wi0", "wi1", T.WI[:, 1:2], T.WI[:, 0:1], 3, A.bitwise_and)
    ts("wi1", "c8", C(8), T.WI[:, 1:2], -1024.0, A.mult, 2049.0, A.add)
    ts("c1", "c9", C(9), C(1), 0.0, A.is_equal, 31.0, A.mult)
    ts("c1", "c10", C(10), C(1), 3.5, A.is_lt)
    tt("c9 c10", "c11", C(11), C(9), C(10), A.add)
    ts("c4", "c14", C(14), C(4), 32.0, A.mult, 31.0, A.add)
    ts("c6", "c15", C(15), C(6), 1000.0, A.mult)
    ts("c6", "c16", C(16), C(6), -1000.0, A.mult, 1000.0, A.add)
    ts("c0", "c17", C(17), C(0), 1.0, A.add)
    ts("c4", "c5", C(5), C(4), 2.0, A.mult)
    ts("c5", "c18", C(18), C(5), 1.0, A.add)
    ts("c3", "c28", C(28), C(3), 1.5, A.is_gt, 1000.0, A.mult)
    ts("c3 c28 c5", "c19", C(19), C(3), C(28), A.add, C(5), A.add)
    ts("c1", "c20", C(20), C(1), 0.0, A.is_equal, 32.0, A.mult)
    ts("RF", "RF2", T.RF2[:], T.RF[:], 3, A.arith_shift_right)
    WT, WF, CS = (T.WT0, T.WT1), (T.WF0, T.WF1), (T.CS0, T.CS1)
    for h in (0, 1):
        tt("c14 c%d" % (15 + h), "c%d" % (21 + h), C(21 + h), C(14), C(15 + h), A.add)
        tt("c4 c%d" % (15 + h), "c%d" % (23 + h), C(23 + h), C(4), C(15 + h), A.add)
        ts("c6", "HM+", T.HM[:, h:h + 1], C(6), float(h), A.is_equal)
        ts("CI c8 c%d" % (21 + h), "WT+", WT[h][:, 0:159], T.CI[:, 0:159], C(21 + h), A.is_equal, C(8), A.mult)
        ts("RF2 c11 c%d" % (23 + h), "WF+", WF[h][:, 0:132], T.RF2[:], C(23 + h), A.is_equal, C(11), A.mult)
    ts("F0", "FH", T.FH[:], T.F0[:], 5, A.logical_shift_right)
    ts("F0", "FD", T.FD[:], T.F0[:], 31, A.bitwise_and)
    ts("c1", "c26", C(26), C(1), 0.0, A.is_equal)
    ts("c1", "c27", C(27), C(1), 1.0, A.is_equal)
    ts("FH c26", "FE", T.FE[:], T.FH[:], C(26), A.mult)
    ts("FD c27", "FG", T.FG[:], T.FD[:], C(27), A.mult)
    for q in range(4):
        tt("FE FG", "XF0c+", T.XF[:, q * 256 + 128:q * 256 + 256], T.FE[:, q * 128:q * 128 + 128], T.FG[:, q * 128:q * 128 + 128], A.add)
    fill("XF1m", T.XF[:, 1024:2048], 0.0)
    for q in range(4):
        x = T.XF[:, 1024 + q * 256 + 128:1024 + q * 256 + 256]
        ts("XF1m c20", "XF1+", x, x, 0.0, A.mult, C(20), A.add)
    fill("FBm", T.FB[:], 0.0)
    ts("FBm c20", "FBz", T.FB[:, 4096:CW], T.FB[:, 4096:CW], 0.0, A.mult, C(20), A.add)
    ci = T.CI[:, 0:128]
    ts("C4 c2", "BO", T.BO[:], T.C4[:], C(2), A.is_equal)
    ts("CL", "TA", T.TMPA[:], T.CL[:], 1.5, A.is_gt)
    ts("CL", "TB", T.TMPB[:], T.CL[:], 3.5, A.is_lt)
    tt("TA TB", "L1", T.LANEG[:], T.TMPA[:], T.TMPB[:], A.mult)
    tt("L1 BO", "TA", T.TMPA[:], T.LANEG[:], T.BO[:], A.mult)
    ts("CL", "TB", T.TMPB[:], T.CL[:], 1.0, A.add)
    tt("TA TB", "L1", T.LANEG[:], T.TMPA[:], T.TMPB[:], A.mult)
    ts("L1", "LANEG", T.LANEG[:], T.LANEG[:], -1.0, A.add)
    ts("C5 c4", "BLK", T.BLK[:], T.C5[:], C(4), A.is_equal)
    ts("BLK", "QALL", T.QALL[:], T.BLK[:], 0.0625, A.mult)
    fill("lo hi last e U", T.ST[:], 0.0)
    fill("last", T.ST[:, 6:9], 1024.0)
    fill("U", T.ST[:, 10:11], 1023.0)
    cp("CI", "I3", T.I3[:, 0:3], T.CI[:, 0:3])
    ts("CI", "J3", T.I3[:, 4:7], T.CI[:, 0:3], 1.0, A.add)
    LO, HI, LA, EE, UU = T.ST[:, 0:3], T.ST[:, 3:6], T.ST[:, 6:9], T.ST[:, 9:10], T.ST[:, 10:11]
    lt = {}

    def L(name, k=1):
        if name not in lt:
            lt[name] = (sum(v[1] for v in lt.values()), k)
        x, k = lt[name]
        return T.LT[:, x:x + k]

    def L1(name, i):
        x = lt[name][0] + i
        return T.LT[:, x:x + 1]

    def derive():
        ts("J3 e", "oh1", L("oh1", 3), T.I3[:, 4:7], EE, A.is_equal)
        ts("e", "e1", L("e1"), EE, 1.0, A.add)
        tt("oh1 last", "sl", L("sl", 3), L("oh1"), LA, A.mult)
        ts("LANEG e1", "TLM", T.TLM[:], T.LANEG[:], L("e1"), A.is_equal)
        red("sl", "slot", L("slot"), L("sl"), A.add)
        ts("e", "e811", L("e811"), EE, 811.0, A.mult)
        ts("PWC slot", "OFS", T.OFS[:], T.PWC[:], L("slot"), A.add)
        tt("oh1 hi", "th", L("th", 3), L("oh1"), HI, A.mult)
        ts("I3 e", "oh", L("oh", 3), T.I3[:, 0:3], EE, A.is_equal)
        red("th", "th1", L("th1"), L("th"), A.add)
        tt("oh lo", "ol", L("ol", 3), L("oh"), LO, A.mult)
        ts("I3 e", "noh", L("noh", 3), T.I3[:, 0:3], EE, A.not_equal)
        ts("oh th1", "thr", L("thr"), L1("oh", 0), 2000.0, A.mult, L("th1"), A.add)
        red("ol", "loe", L("loe"), L("ol"), A.add)
        ts("HM thr", "RH2", T.RH[:, 2:4], T.HM[:], L("thr"), A.mult)
        ts("HM loe", "RH0", T.RH[:, 0:2], T.HM[:], L("loe"), A.mult)

    derive()

    def search_constants():
        ts("CI c0", "IDENT", T.IDENT[:], ci, C(0), A.is_equal)
        ts("CI c4", "SEL4", T.SEL4[:, 0:4], T.CI[:, 0:4], C(4), A.is_equal)
        ts("CM3 c4", "MASKG", T.MASKG[:], T.CM3[:], C(4), A.not_equal, -8192.0, A.mult)
        fill("ONES", T.ONES[:], 1.0)
        fill("MTm", T.MT[:], 3000.0)

    late = [lambda: ts("CI c0", "TA", T.TMPA[:], ci, C(0), A.is_gt),
            lambda: ts("CI c17", "TB", T.TMPB[:], ci, C(17), A.is_equal),
            lambda: fill("RSTm", T.RST[:], 1.0),
            lambda: tt("TA BLK", "TRI", T.TRI[:], T.TMPA[:], T.BLK[:], A.mult),
            lambda: tt("TB BLK", "SHIFT", T.SHIFT[:], T.TMPB[:], T.BLK[:], A.mult),
            lambda: V(lambda e: e.memset(T.RST[:, 0::128], 0.0), "RSTm", "RST"),
            lambda: tt("IDENT SHIFT", "IMS", T.IMS[:], T.IDENT[:], T.SHIFT[:], A.subtract),
            lambda: ts("C4 c5", "CS", T.CS0[:], T.C4[:], C(5), A.is_equal),
            lambda: ts("C4 c18", "CS+", T.CS1[:], T.C4[:], C(18), A.is_equal),
            lambda: ts("C4 c19", "CM", T.CM[:], T.C4[:], C(19), A.is_equal),
            lambda: fill("CHz", T.CH[:, 4096:CW], 0.0),
            lambda: ts("CI c1", "LQ", T.LQ[:], T.CI[:, 0:16], C(1), A.is_equal, 128.0, A.mult)]
    late += [lambda q=q: fill("BMo%d" % q, T.BML[:, q * 16 + rank * 4:q * 16 + rank * 4 + 4], 0.0) for q in range(RO)]
    late += [lambda q=q: ts("CI c0 LQ", "DIAG+", T.DIAG[:, q * 128:(q + 1) * 128], ci, C(0), A.is_equal, T.LQ[:, q:q + 1], A.mult)
             for q in range(16)]

    def output_constants():
        for l in (1, 2, 3):
            fill("OS%d" % l, T["OS%d" % l][:], 0.0)
            fill("OV%d" % l, T["OV%d" % l][:], 1023.0)
        ts("C4 c2", "BCF", T.BCF[:], T.C4[:], C(2), A.is_equal, C(11), A.mult)
        ts("PW1 c1", "PW1", T.PW1[:], T.PW1[:], C(1), A.add, -128.0, A.mult)
        ts("PW2 c1", "PW2", T.PW2[:], T.PW2[:], C(1), A.add, 512.0, A.add)
        ts("PW1", "K1", T.K1[:], T.PW1[:], -513.0 * 128, A.add)
        ts("PW2", "K2", T.K2[:], T.PW2[:], 16384.0, A.mult)

    xkeys = ["XF0s", "XF0c", "XF1"]
    SE = T.SELC
    for r in range(RO):
        win = (r + 2) * 1024
        xk = " ".join(xkeys)
        cp(xk + " OFS", "SS", T.SS[:], T.XF[:, 0:win].indirect(T.OFS[:]))
        act(xk + " OFS", "SF", T.SF[:], T.XF[:, 128:win].indirect(T.OFS[:]), F.Copy)
        for q in range(16):
            mm("WMARK SS", "ps3", b(3, 0, 32), T.WMARK[:, 15 - q:143 - q], T.SS[:, q::16], q == 0, q == 15)
        mm("TLM SS", "ps4", b(4, 0, 512), T.TLM[:], T.SS[:])
        u = [T.UI[:, k * 32:(k + 1) * 32] for k in range(4)]
        cp("ps3", "u0", u[0], b(3, 0, 32))
        ts("u0", "u1", u[1], u[0], 4095, A.bitwise_and)
        tt("u1", "u2", u[2], u[1], u[1], A.mult)
        cp("u1", "uf0", T.UF[:, 0:32], u[1])
        ts("u2", "u3", u[3], u[2], 4, A.logical_shift_right, 8191, A.bitwise_and)
        tt("uf0 REP KMAT", "KU", T.KU[:], T.UF[:, 0:32].indirect(T.REP[:]), T.KMAT[:], A.mult)
        ts("u3 e811", "uf1", T.UF[:, 32:64], u[3], L("e811"), A.add)
        tt("uf1 REP KU", "OFP", T.OFP[:], T.UF[:, 32:64].indirect(T.REP[:]), T.KU[:], A.add)
        ts("OFP", "OFM", T.OFM[:], T.OFP[:], 8191, A.bitwise_and)
        cp("OFM", "OFU", T.OFU[:], T.OFM[:])
        mm("QALL RH0 RH2", "ps3", b(3, 40, 44), T.QALL[:], T.RH[:])
        for j in range(8):
            d = T.DY[:, j * 512:(j + 1) * 512]
            tt("OPS OFU SS", "DY%d" % j, d, T.OPS[:].indirect(T.OFU[:, j * 32:(j + 1) * 32]), T.SS[:], A.subtract)
            act("DY%d" % j, "CH%d" % j, T.CH[:, j * 512:(j + 1) * 512], d, F.Abs)
            for co in range(4 * j, 4 * j + 4):
                for h in (0, 1):
                    mm("WT CH%d" % j, "ps%d" % h, b(h, 0, 128), WT[h][:, 31 - co:159 - co], T.CH[:, co * 128:(co + 1) * 128], co == 0, co == 31)
            if j == 0:
                ts("ps4", "FL", T.FL[:], b(4, 0, 512), 0.25, A.mult, -0.375, A.add)
                tt("SF FL FBm", "FB", T.FB[:, 0:512], T.SF[:], T.FL[:], A.add)
                for h in (0, 1):
                    for m in range(4):
                        mm("WF FB", "ps2", b(2, h * 128, h * 128 + 128), WF[h][:, 3 - m:131 - m], T.FB[:, m * 128:(m + 1) * 128], m == 0, m == 3)
                cp("ps3", "TS", T.TS[:], b(3, 40, 44))
            if j == 3:
                for h in (0, 1):
                    ts("ps2 TS", "PEN+", T.PEN[:, h * 128:h * 128 + 128], b(2, h * 128, h * 128 + 128), T.TS[:, 2 + h:3 + h], A.is_ge, 4000.0, A.mult)
                tt("ps2 PEN", "ps5", b(5, 0, 256), b(2, 0, 256), T.PEN[:], A.add)
        if r == 0:
            search_constants()
        for h in (0, 1):
            cp("ps%d" % h, "I1+", T.I1[:, h * 128:h * 128 + 128], b(h, 0, 128))
        ts("I1", "OW", T.OW[:], T.I1[:], 10, A.arith_shift_right, 3, A.bitwise_and)
        ts("I1", "T4", T.T4[:], T.I1[:], 1023, A.bitwise_and, 2, A.logical_shift_right)
        cp("OW", "OWF", T.OWF[:], T.OW[:])
        for o in range(4):
            k = 4 if o < 2 else 2
            act("OWF", "ps%d" % k, b(k, (o % 2) * 256, (o % 2) * 256 + 256), T.OWF[:], F.Square, bias=-64.0 * o, scale=64.0)
        tt("T4 ps5", "CC", T.CC[:], T.T4[:], b(5, 0, 256), A.add)
        for h in (0, 1):
            ts("CC TS", "ps5", b(5, 256 + h * 128, 384 + h * 128), T.CC[:, h * 128:h * 128 + 128], T.TS[:, h:h + 1], A.is_lt, 4000.0, A.mult)
        tt("CC ps5", "CP", T.CP[:], T.CC[:], b(5, 256, 512), A.add)
        for h in (0, 1):
            for o in range(4):
                k = 4 if o < 2 else 2
                x = (o % 2) * 256 + h * 128
                tt("CP ps%d" % k, "KEY%d+" % h, T.KEY[:, h * 512 + o * 128:h * 512 + (o + 1) * 128], T.CP[:, h * 128:h * 128 + 128], b(k, x, x + 128), A.add)

        def dl(h, s):
            return SE[:, h * 32 + s:h * 32 + s + 1]

        def bs(h, s):
            return SE[:, h * 32 + 10 + s:h * 32 + 11 + s]

        def vi(h, s):
            return SE[:, h * 32 + 21 + s:h * 32 + 22 + s]

        for s in range(11):
            bit = 512 >> s
            for h in (0, 1):
                ky, io = T.KEY[:, h * 512:(h + 1) * 512], T.IN0[:, h * 512:(h + 1) * 512]
                if s > 0:
                    ts("v%d.%d" % (h, s - 1), "d%d.%d" % (h, s - 1), dl(h, s - 1), vi(h, s - 1), 0.5, A.is_lt, float(512 >> (s - 1)), A.mult)
                if s == 0:
                    ts("KEY%d" % h, "IN0%d" % h, io, ky, 512.0, A.is_lt)
                elif s == 1:
                    ts("KEY%d d%d.0" % (h, h), "IN0%d" % h, io, ky, dl(h, 0), A.subtract, 256.0, A.is_lt)
                else:
                    ts("KEY%d d%d.%d b%d.%d" % (h, h, s - 1, h, s), "IN0%d" % h, io, ky, dl(h, s - 1), A.subtract, bs(h, s), A.is_lt)
                if s == 10:
                    continue
                k = 6 + h
                pk = "ps%d" % k
                for o in range(4):
                    mm("IN0%d SEL4" % h, pk, b(k, o * 4, o * 4 + 4), T.IN0[:, h * 512 + o * 128:h * 512 + (o + 1) * 128], T.SEL4[:, 0:4])
                act(pk, "CN%d" % h, T.CN[:, h * 16:h * 16 + 16], b(k, 0, 16), F.Copy)
                mm("IDENT MASKG", pk, b(k, 32, 48), T.IDENT[:], T.MASKG[:], True, False)
                mm("ONES CN%d" % h, pk, b(k, 32, 48), T.ONES[:], T.CN[:, h * 16:h * 16 + 16], False, True)
                act(pk, "SG%d v%d.%d" % (h, h, s), T.SG[:, h * 16:h * 16 + 16], b(k, 32, 48), F.Sigmoid, bias=-128.5 * 64, scale=64.0, accum_out=vi(h, s))
            if s == 0:
                for h in (0, 1):
                    red("CP MTm", "MT+", T.MT[:, h:h + 1], T.CP[:, h * 128:h * 128 + 128], A.min)
                V(lambda e: e.transpose(T.MTT[:], T.MT[:]), "MT MTm", "MTT")
                red("MTT", "MM0", T.MM[:, 0:1], T.MTT[:], A.min)
                ts("MM0", "BHm", T.BH[:, 2:3], T.MM[:, 0:1], 2000.0, A.min)
            for h in (0, 1):
                if s == 1:
                    ts("d%d.0" % h, "b%d.2" % h, bs(h, 2), dl(h, 0), 128.0, A.add)
                elif 2 <= s < 10:
                    ts("b%d.%d d%d.%d" % (h, s, h, s - 1), "b%d.%d" % (h, s + 1), bs(h, s + 1), bs(h, s), dl(h, s - 1), A.add,
                       float((bit >> 1) - bit), A.add)
            for _ in range(4):
                if s and late:
                    late.pop(0)()
        for h in (0, 1):
            scan("RST IN0%d" % h, "SC%d" % h, T.SC[:, h * 512:(h + 1) * 512], T.IN0[:, h * 512:(h + 1) * 512])
        for h in (0, 1):
            ts("d%d.9 b%d.10" % (h, h), "BHb%d" % h, T.BH[:, h:h + 1], dl(h, 9), bs(h, 10), A.add, 0.03125, A.mult)
        tot = T.SC[:, 127:1024:128]
        mm("TRI SC0 SC1", "ps3", b(3, 64, 72), T.TRI[:], tot)
        mm("SHIFT SC0 SC1", "ps3", b(3, 72, 80), T.SHIFT[:], tot)
        for h in (0, 1):
            mm("IMS SC%d" % h, "ps%d" % (6 + h), b(6 + h, 0, 512), T.IMS[:], T.SC[:, h * 512:(h + 1) * 512])
        for h in (0, 1):
            mm("CS BHb%d" % h, "ps5", b(5, 0, 1), CS[h][:], T.BH[:, h:h + 1], h == 0, h == 1)
        mm("CM BHm", "ps5", b(5, 1, 2), T.CM[:], T.BH[:, 2:3])
        cp("ps3", "SP", T.SP[:], b(3, 64, 80))
        x = r * 16 + rank * 4
        own = T.BML[:, x:x + 4]
        cp("ps5", "BMo%d" % r, T.BML[:, x:x + 2], b(5, 0, 2))
        send("bm", r, "lsb", lambda q: own, own, "BMo%d" % r)
        for o in range(4):
            ho = o * 128
            act("ps6 SP", "DD0%d" % o, T.DD[:, ho:ho + 128], b(6, ho, ho + 128), F.Identity, bias=T.SP[:, 8 + o:9 + o])
            for h in (0, 1):
                ts("KK SP", "STEP%d%d" % (h, o), T.STEP[:, h * 512 + ho:h * 512 + ho + 128], T.KK[:, 0:128], T.SP[:, h * 4 + o:h * 4 + o + 1], A.is_ge)
            ts("ps7 SP", "DD1%d" % o, T.DD[:, 512 + ho:640 + ho], b(7, ho, ho + 128), T.SP[:, 12 + o:13 + o], A.add)

        def place(ph, q):
            k = (0, 1, 4, 5)[q]
            for o in (2 * ph, 2 * ph + 1):
                for h in (0, 1):
                    ho, x = h * 512 + o * 128, (o % 2) * 256 + h * 128
                    mm("DD%d%d STEP%d%d" % (h, o, h, o), "ps%d" % k, b(k, x, x + 128), T.DD[32 * q:32 * q + 32, ho:ho + 128],
                       T.STEP[32 * q:32 * q + 32, ho:ho + 128])
            for o in (2 * ph, 2 * ph + 1):
                x = o * 1024 + q * 256
                tt("ps%d KK" % k, "IND%d+" % o, T.IND[:, x:x + 256], b(k, (o % 2) * 256, (o % 2) * 256 + 256), T.KK[:, 0:256], A.is_le)

        def wrap(o):
            for a in range(8):
                c = 96 + a * 4 + o
                mm("IND%d ONES" % o, "ps3", b(3, c, c + 1), T.IND[:, o * 1024 + a:(o + 1) * 1024:8], T.ONES[:, 0:1], False, o == 3 and a == 7)

        for q in range(4):
            place(0, q)
        for a in range(8):
            for h in (0, 1):
                mm("CS " + " ".join("STEP%d%d" % (h, o) for o in range(4)), "ps2", b(2, a * 64, a * 64 + 64), CS[h][:],
                   T.STEP[:, h * 512 + a:(h + 1) * 512:8], h == 0, h == 1)
        act("ps2", "CCR", T.CCR[:], b(2, 0, 512), F.Copy)
        for q in range(4):
            place(1, q)
        for q in range(16):
            mm("DIAG CCR", "ps3", b(3, 96, 128), T.DIAG[:, q * 128:(q + 1) * 128], T.CCR[:, q::16], q == 0, False)
        for o in range(4):
            wrap(o)
        bk = "BMo%d bm%d" % (r, r)
        red(bk, "B", L("B"), T.BML[:, r * 16:r * 16 + 16:4], A.min)
        red(bk, "M", L("M"), T.BML[:, r * 16 + 1:r * 16 + 16:4], A.min)
        tt("hi noh", "ha", L("ha", 3), HI, L("noh"), A.mult)
        tt("last noh", "la", L("la", 3), LA, L("noh"), A.mult)
        ts("oh", "lb", L("lb", 3), L("oh"), float((r + 2) * 1024), A.mult)
        ts("M B", "kept", L("kept"), L("M"), L("B"), A.is_lt)
        ts("oh B", "hb", L("hb", 3), L("oh"), L("B"), A.mult)
        ts("loe B", "x", L("x"), L("loe"), 1.0, A.add, L("B"), A.max)
        ts("kept oh", "k2", L("k2"), L("kept"), L1("oh", 2), A.mult, -4000.0, A.mult)
        tt("la lb", "last", LA, L("la"), L("lb"), A.add)
        tt("ha hb", "hi", HI, L("ha"), L("hb"), A.add)
        ts("k2 M", "uc", L("uc"), L("k2"), L("M"), A.add, 4000.0, A.add)
        tt("uc U", "U", UU, UU, L("uc"), A.min)
        for o in range(4):
            ts("ps3", "LI+", T.LI[:, o * 8:o * 8 + 8], b(3, 96 + o, 128, 4), -128.0, A.add)
        cp("LI", "LU", T.LU[:], T.LI[:, 0:32])
        ts("LI", "LI2", T.LI[:, 32:64], T.LI[:, 0:32], 4607, A.bitwise_and)
        cp("LI2", "LCU", T.LCU[:], T.LI[:, 32:64])
        xo = (r + 2) * 1024 + rank * 256
        chk = " ".join("CH%d" % j for j in range(8)) + " CHz LU"
        for o in sorted(range(4), key=lambda o: o == rank):
            t, x, kk = (T.XF, xo, "XO%d" % r) if o == rank else (T.MSG, o * 256, "MSG")
            cp(chk, kk + "s+", t[:, x:x + 128], T.CH[:].indirect(T.LU[:, o * 8:o * 8 + 8]))
            act("FB FBm FBz LCU", kk + "c+", t[:, x + 128:x + 256], T.FB[:].indirect(T.LCU[:, o * 8:o * 8 + 8]), F.Copy)
        send("dat", r, "lsd", lambda q: T.MSG[:, q * 256:(q + 1) * 256], T.XF[:, xo:xo + 256], "MSGs MSGc")
        xkeys += ["XO%ds" % r, "XO%dc" % r, "dat%d" % r]
        ts("M U", "ml", L("ml"), L("M"), UU, A.is_lt)
        ts("x U", "xu", L("xu"), L("x"), UU, A.is_ge)
        ts("ml kept noh", "adv0", L("adv0"), L("ml"), L("kept"), A.mult)
        ts("adv0 noh", "adv", L("adv"), L("adv0"), L1("noh", 2), A.mult)
        ts("adv", "nadv", L("nadv"), L("adv"), -1.0, A.mult, 1.0, A.add)
        ts("xu noh nadv", "back", L("back"), L("xu"), L1("noh", 0), A.mult, L("nadv"), A.mult)
        ts("adv e back", "e", EE, L("adv"), EE, A.add, L("back"), A.subtract)
        ts("back", "nb", L("nb"), L("back"), -1.0, A.mult, 1.0, A.add)
        ts("adv loe", "al", L("al"), L("adv"), L("loe"), A.mult)
        tt("lo noh", "lo0", L("lo0", 3), LO, L("noh"), A.mult)
        ts("x nadv nb", "y", L("y"), L("x"), L("nadv"), A.mult, L("nb"), A.mult)
        ts("I3 e", "oq", L("oq", 3), T.I3[:, 0:3], EE, A.is_equal)
        ts("adv back", "ch", L("ch"), L("adv"), L("back"), A.add)
        tt("al y", "z", L("z"), L("al"), L("y"), A.add)
        ts("oq back", "tb", L("tb", 3), L("oq"), L("back"), A.mult)
        ts("oq ch", "tk", L("tk", 3), L("oq"), L("ch"), A.mult)
        ts("oh z", "oz", L("oz", 3), L("oh"), L("z"), A.mult)
        ts("tk", "tn", L("tn", 3), L("tk"), -1.0, A.mult, 1.0, A.add)
        tt("lo0 oz", "l1", L("l1", 3), L("lo0"), L("oz"), A.add)
        ts("l1", "l2", L("l2", 3), L("l1"), 1.0, A.add)
        tt("l1 tn", "l3", L("l3", 3), L("l1"), L("tn"), A.mult)
        tt("l2 hi", "l4", L("l4", 3), L("l2"), HI, A.max)
        tt("l4 tb", "l5", L("l5", 3), L("l4"), L("tb"), A.mult)
        tt("l3 l5", "lo", LO, L("l3"), L("l5"), A.add)
        if r + 1 < RO:
            derive()
        if r == 0:
            output_constants()

    xk = " ".join(xkeys)
    win = NSLOT * 1024
    cp("lo hi", "YT", T.YT[:, 0:6], T.ST[:, 0:6])
    cp("e U", "YT+", T.YT[:, 6:8], T.ST[:, 9:11])
    dma("Y", "out", [(T.yt[:], T.YT[0::16, :])], "YT", "yt")
    for l in (1, 2, 3):
        ts("PWC last", "FO%d" % l, T["FO%d" % l][:, 0:32], T.PWC[:], T.ST[:, 5 + l:6 + l], A.add)
    for l in (1, 2, 3):
        off = T["FO%d" % l][:, 0:32]
        cp(xk + " FO%d" % l, "FS%d" % l, T["FS%d" % l][:], T.XF[:, 0:win].indirect(off))
        act(xk + " FO%d" % l, "FC%d" % l, T["FC%d" % l][:], T.XF[:, 128:win].indirect(off), F.Copy)
        mm("BO FS%d" % l, "ps%d" % l, b(l, 0, 512), T.BO[:], T["FS%d" % l][:])
        mm("BCF FC%d" % l, "ps%d" % (3 + l), b(3 + l, 0, 512), T.BCF[:], T["FC%d" % l][:])
    for l in (1, 2, 3):
        fv, fa, fn = T["FV%d" % l][:], T["FA%d" % l][:], T["FN%d" % l][:]
        ts("ps%d" % l, "FL", T.FL[:], b(l, 0, 512), 0.25, A.mult, -0.375, A.add)
        tt("FL ps%d" % (3 + l), "FV%d" % l, fv, T.FL[:], b(3 + l, 0, 512), A.add)
        ts("FV%d hi" % l, "FA%d" % l, fa, fv, T.ST[:, 2 + l:3 + l], A.is_lt)
        scan("RST FA%d" % l, "FN%d" % l, fn, fa)
        k = (7, 0, 3)[l - 1]
        for i, t in enumerate((fn, fa)):
            t = T[("FN%d", "FA%d")[i] % l]
            for q in range(16):
                mm("DIAG F%s%d" % ("NA"[i], l), "ps%d" % k, b(k, i * 32, i * 32 + 32), T.DIAG[:, q * 128:(q + 1) * 128], t[:, q::16], q == 0, q == 15)
    for l in (1, 2, 3):
        k = (7, 0, 3)[l - 1]
        fo = T["FO%d" % l][:, 32:64]
        w1, w2 = T.WX[:, l * 64 - 64:l * 64 - 32], T.WX[:, l * 64 - 32:l * 64]
        tt("ps%d K1" % k, "w1%d" % l, w1, b(k, 0, 32), T.K1[:], A.add)
        tt("ps%d w1%d" % (k, l), "w2%d" % l, w2, b(k, 32, 64), w1, A.mult)
        tt("w2%d K2" % l, "w1%d" % l, w1, w2, T.K2[:], A.add)
        ts("w1%d" % l, "FP%d" % l, fo, w1, 1.0 / 16384, A.mult)
        o1, o2 = T["OS%d" % l], T["OV%d" % l]
        cp("FP%d FS%d OS%d" % (l, l, l), "OS%d" % l, o1[:].indirect(fo), T["FS%d" % l][:])
        dma("Y", "out", [(T.yl[:, (l - 1) * 512:l * 512], o1[:, 0:512])], "OS%d" % l, "yl%d" % l)
        cp("FP%d FV%d OV%d" % (l, l, l), "OV%d" % l, o2[:].indirect(fo), T["FV%d" % l][:])
        dma("Y", "out", [(T.yf[:, (l - 1) * 512:l * 512], o2[0::16, 0:512])], "OV%d" % l, "yf%d" % l)
    need("G", list(cnt.items()) + [("%s%d" % (s, r), arrive) for s in ("bm", "dat") for r in range(RO)])
